import numpy as np, ml_dtypes
CORES = [10,18,34,42,58,66,82,90,98,106]
N = 10
KB, QP = 1, 32
MEM = [3,7]
def setup_inputs(rng):
    return {"q": rng.standard_normal((N, 128, QP), dtype=np.float32).astype(ml_dtypes.bfloat16), "k": rng.standard_normal((N, 128, KB * 128), dtype=np.float32).astype(ml_dtypes.bfloat16), "v": rng.standard_normal((N, 128, KB * 128), dtype=np.float32).astype(ml_dtypes.bfloat16)}
def setup_inputs_big(rng):
    d = setup_inputs(rng)
    for k in ("q", "k", "v"): d[k] = (d[k].astype(np.float32) * 1024.0).astype(d[k].dtype)
    return d
def setup_inputs_small(rng):
    d = setup_inputs(rng)
    for k in ("q", "k", "v"): d[k] = (d[k].astype(np.float32) * (1 / 1024.0)).astype(d[k].dtype)
    return d
def setup_inputs_apart(rng):
    d = setup_inputs(rng)
    f = (10.0 ** rng.permutation(np.linspace(-1.5, 1.5, N))).astype(np.float32).reshape(N, 1, 1)
    for k in ("q", "k", "v"): d[k] = (d[k].astype(np.float32) * f).astype(d[k].dtype)
    return d
def reference(q, k, v):
    Q, K, V = q.astype(np.float64), k.astype(np.float64), v.astype(np.float64)
    y = np.zeros((N, 128, QP))
    for r in range(N):
        for j in MEM:
            for b in range(KB):
                S = np.maximum(K[j][:, 128 * b:128 * b + 128].T @ Q[r], 0.0)
                y[r] += V[j][:, 128 * b:128 * b + 128].T @ S
    return {"y": y.astype(ml_dtypes.bfloat16 if q.dtype != np.float64 else np.float64)}

@@ -1,0 +1,161 @@
+from concourse.bass import DstId, RemoteDMATransfer
+from concourse.mybir import AluOpType
+
+QP = 32
+KP = 128
+GUESTS = 4
+GW = GUESTS * QP
+W = GW + QP
+
+SCRATCH = {
+    "qd": ("dram", [128, QP], "bfloat16"),
+    "oland": ("dram", [128, QP], "bfloat16"),
+    "kv": ("sbuf", [128, 2 * KP], "bfloat16"),
+    "kvo": ("sbuf", [128, 2 * KP], "bfloat16"),
+    "Q": ("sbuf", [128, W], "bfloat16"),
+    "zero": ("sbuf", [128, W], "float32"),
+    "S1": ("sbuf", [128, W], "bfloat16"),
+    "S2": ("sbuf", [128, W], "bfloat16"),
+    "Ob": ("sbuf", [128, GW], "bfloat16"),
+    "Oown": ("sbuf", [128, QP], "bfloat16"),
+    "P1": ("psum", [128, 512], "float32"),
+    "P2": ("psum", [128, 512], "float32"),
+    "P3": ("psum", [128, 512], "float32"),
+}
+SEMAPHORES = ["ldkv", "ldq", "qarr", "kvarr", "oarr", "sent", "st",
+              "zs", "m1", "m2", "m3", "r1", "r2", "c1", "c2"]
+
+
+def _engines(mask):
+    return [b for b in range(mask.bit_length()) if (mask >> b) & 1]
+
+
+def _bits(engines):
+    m = 0
+    for b in engines:
+        m |= 1 << b
+    return m
+
+
+def _pow2_floor(n):
+    p = 1
+    while 2 * p <= n:
+        p *= 2
+    return p
+
+
+def _hops(topo, a, b):
+    ca, cb = topo.chip(a), topo.chip(b)
+    if ca == cb:
+        return 0
+    if topo.mates(ca, cb) or topo.same_plane(ca, cb):
+        return 1
+    return 2
+
+
+def _plan(T, topo):
+    hubs = [T.cores[j] for j in T.tables["MEM"]]
+    guests = {h: [] for h in hubs}
+    rest = [c for c in T.cores if c not in hubs]
+    near = [c for c in rest if len({_hops(topo, c, h) for h in hubs}) > 1]
+    for c in near:
+        guests[min(hubs, key=lambda h: _hops(topo, c, h))].append(c)
+    even = sorted([c for c in rest if c not in near], key=lambda c: _hops(topo, c, hubs[0]))
+    for c in even:
+        guests[min(hubs, key=lambda h: len(guests[h]))].append(c)
+    return hubs, guests
+
+
+def _check(topo, src, dst):
+    if not topo.may_write(src, dst):
+        raise ValueError("core %d may not write to core %d" % (src, dst))
+
+
+def _guest(g, core, T, topo, hub, slot):
+    _check(topo, core, hub)
+    rid, pid, _ = topo.addr(hub)
+    mask = topo.mask(core, hub)
+    n = len(_engines(mask))
+    g.sync.dma_start(T.qd[:], T.q[:]).then_inc(T.sem.ldq, 16)
+    g.wait_ge(T.sem.ldq, 16)
+    g.remote_dma(T.Q[:, slot * QP:(slot + 1) * QP], T.qd[:], T.sem.qarr, T.sem.sent, pid, rid, mask)
+    back = _return_engines(topo, hub, [core])
+    g.sync.wait_ge(T.sem.oarr, back)
+    g.sync.dma_start(T.y[:], T.oland[:]).then_inc(T.sem.st, 16)
+    g.sync.wait_ge(T.sem.st, 16)
+    g.wait_ge(T.sem.sent, n)
+
+
+def _return_engines(topo, hub, dsts):
+    return _pow2_floor(len(_engines(topo.mask(hub, dsts[0]))) // GUESTS)
+
+
+def _hub(g, core, T, topo, other, guests):
+    s = T.sem
+    _check(topo, core, other)
+    g.sync.dma_start(T.kv[:, 0:KP], T.k[:]).then_inc(s.ldkv, 16)
+    g.scalar.dma_start(T.kv[:, KP:2 * KP], T.v[:]).then_inc(s.ldkv, 16)
+    g.sync.dma_start(T.Q[:, GW:W], T.q[:]).then_inc(s.ldq, 16)
+    g.vector.memset(T.zero[:], 0.0).then_inc(s.zs, 1)
+
+    rid, pid, _ = topo.addr(other)
+    mask = topo.mask(core, other)
+    n_kv = len(_engines(mask))
+    g.wait_ge(s.ldkv, 32)
+    g.remote_dma(T.kvo[:], T.kv[:], s.kvarr, s.sent, pid, rid, mask)
+
+    n_q = sum(len(_engines(topo.mask(c, core))) for c in guests)
+    te = g.tensor
+    te.wait_ge(s.ldkv, 32)
+    te.wait_ge(s.ldq, 16)
+    te.wait_ge(s.qarr, n_q)
+    te.matmul(T.P1[:, 0:W], T.kv[:, 0:KP], T.Q[:], True, True).then_inc(s.m1, 1)
+    te.wait_ge(s.kvarr, len(_engines(topo.mask(other, core))))
+    te.matmul(T.P2[:, 0:W], T.kvo[:, 0:KP], T.Q[:], True, True).then_inc(s.m2, 1)
+    te.wait_ge(s.r1, 1)
+    te.matmul(T.P3[:, 0:W], T.kv[:, KP:2 * KP], T.S1[:], True, False)
+    te.wait_ge(s.r2, 1)
+    te.matmul(T.P3[:, 0:W], T.kvo[:, KP:2 * KP], T.S2[:], False, True).then_inc(s.m3, 1)
+
+    ve = g.vector
+    ve.wait_ge(s.zs, 1)
+    ve.wait_ge(s.m1, 1)
+    ve.tensor_tensor(T.S1[:], T.P1[:, 0:W], T.zero[:], AluOpType.max).then_inc(s.r1, 1)
+    ve.wait_ge(s.m2, 1)
+    ve.tensor_tensor(T.S2[:], T.P2[:, 0:W], T.zero[:], AluOpType.max).then_inc(s.r2, 1)
+    ve.wait_ge(s.m3, 1)
+    ve.tensor_copy(T.Ob[:], T.P3[:, 0:GW]).then_inc(s.c1, 1)
+    ve.tensor_copy(T.Oown[:], T.P3[:, GW:W]).then_inc(s.c2, 1)
+
+    common = topo.mask(core, guests[0])
+    for c in guests:
+        _check(topo, core, c)
+        common &= topo.mask(core, c)
+    engines = _engines(common)
+    per = _return_engines(topo, core, guests)
+    transfers = []
+    for i, c in enumerate(guests):
+        rid, pid, _ = topo.addr(c)
+        transfers.append(RemoteDMATransfer(dst_ids=[DstId(rid=rid, pnc=pid)],
+                                           dma_engine_mask=_bits(engines[i * per:(i + 1) * per]),
+                                           remote_sem=s.oarr,
+                                           src=T.Ob[:, i * QP:(i + 1) * QP], dst=T.oland[:]))
+    g.wait_ge(s.c1, 1)
+    g.remote_dma_fused(transfers, local_sem=s.sent)
+
+    g.sync.wait_ge(s.c2, 1)
+    g.sync.dma_start(T.y[:], T.Oown[:]).then_inc(s.st, 16)
+    g.sync.wait_ge(s.st, 16)
+    g.wait_ge(s.sent, n_kv + per * len(guests))
+
+
+def rank_program(g, core, T, topo):
+    if T.rank_of(core) is None:
+        return
+    hubs, guests = _plan(T, topo)
+    if core in hubs:
+        _hub(g, core, T, topo, hubs[1 - hubs.index(core)], guests[core])
+    else:
+        for h in hubs:
+            if core in guests[h]:
+                _guest(g, core, T, topo, h, guests[h].index(core))

@@ -4,26 +4,38 @@ from concourse.mybir import AluOpType
 QP = 32
 KP = 128
 GUESTS = 4
+PART = GUESTS // 2
 GW = GUESTS * QP
-W = GW + QP
+H = GW // 2
 
 SCRATCH = {
     "qd": ("dram", [128, QP], "bfloat16"),
     "oland": ("dram", [128, QP], "bfloat16"),
-    "kv": ("sbuf", [128, 2 * KP], "bfloat16"),
-    "kvo": ("sbuf", [128, 2 * KP], "bfloat16"),
-    "Q": ("sbuf", [128, W], "bfloat16"),
-    "zero": ("sbuf", [128, W], "float32"),
-    "S1": ("sbuf", [128, W], "bfloat16"),
-    "S2": ("sbuf", [128, W], "bfloat16"),
-    "Ob": ("sbuf", [128, GW], "bfloat16"),
+    "kd": ("dram", [128, KP], "bfloat16"),
+    "ko": ("sbuf", [128, KP], "bfloat16"),
+    "vo": ("sbuf", [128, KP], "bfloat16"),
+    "kx": ("sbuf", [128, KP], "bfloat16"),
+    "vx": ("sbuf", [128, KP], "bfloat16"),
+    "Q": ("sbuf", [128, GW], "bfloat16"),
+    "Qo": ("sbuf", [128, QP], "bfloat16"),
+    "zero": ("sbuf", [128, GW], "float32"),
+    "S1": ("sbuf", [128, GW], "bfloat16"),
+    "S2a": ("sbuf", [128, H], "bfloat16"),
+    "S2b": ("sbuf", [128, H], "bfloat16"),
+    "So": ("sbuf", [128, 2 * QP], "bfloat16"),
+    "Oa": ("sbuf", [128, H], "bfloat16"),
+    "Obb": ("sbuf", [128, H], "bfloat16"),
     "Oown": ("sbuf", [128, QP], "bfloat16"),
     "P1": ("psum", [128, 512], "float32"),
-    "P2": ("psum", [128, 512], "float32"),
-    "P3": ("psum", [128, 512], "float32"),
+    "P2a": ("psum", [128, 512], "float32"),
+    "P2b": ("psum", [128, 512], "float32"),
+    "P3a": ("psum", [128, 512], "float32"),
+    "P3b": ("psum", [128, 512], "float32"),
+    "P5": ("psum", [128, 512], "float32"),
+    "P6": ("psum", [128, 512], "float32"),
 }
-SEMAPHORES = ["ldkv", "ldq", "qarr", "kvarr", "oarr", "sent", "st",
-              "zs", "m1", "m2", "m3", "r1", "r2", "c1", "c2"]
+SEMAPHORES = ["ldkd", "ldk", "ldv", "ldq", "qarr", "karr", "varr", "oarr", "sent", "st", "zs",
+              "m1", "m2a", "m2b", "m3a", "m3b", "m5", "m6", "r1", "r2a", "r2b", "r5", "c1a", "c1b", "c2"]
 
 
 def _engines(mask):
@@ -63,6 +75,8 @@ def _plan(T, topo):
     even = sorted([c for c in rest if c not in near], key=lambda c: _hops(topo, c, hubs[0]))
     for c in even:
         guests[min(hubs, key=lambda h: len(guests[h]))].append(c)
+    for h in hubs:
+        guests[h].sort(key=lambda c: -_hops(topo, c, h))
     return hubs, guests
 
 
@@ -71,82 +85,103 @@ def _check(topo, src, dst):
         raise ValueError("core %d may not write to core %d" % (src, dst))
 
 
+def _return_engines(topo, hub, dst):
+    return _pow2_floor(len(_engines(topo.mask(hub, dst))) // PART)
+
+
 def _guest(g, core, T, topo, hub, slot):
     _check(topo, core, hub)
     rid, pid, _ = topo.addr(hub)
     mask = topo.mask(core, hub)
-    n = len(_engines(mask))
     g.sync.dma_start(T.qd[:], T.q[:]).then_inc(T.sem.ldq, 16)
     g.wait_ge(T.sem.ldq, 16)
     g.remote_dma(T.Q[:, slot * QP:(slot + 1) * QP], T.qd[:], T.sem.qarr, T.sem.sent, pid, rid, mask)
-    back = _return_engines(topo, hub, [core])
-    g.sync.wait_ge(T.sem.oarr, back)
+    g.sync.wait_ge(T.sem.oarr, _return_engines(topo, hub, core))
     g.sync.dma_start(T.y[:], T.oland[:]).then_inc(T.sem.st, 16)
     g.sync.wait_ge(T.sem.st, 16)
-    g.wait_ge(T.sem.sent, n)
-
-
-def _return_engines(topo, hub, dsts):
-    return _pow2_floor(len(_engines(topo.mask(hub, dsts[0]))) // GUESTS)
+    g.wait_ge(T.sem.sent, len(_engines(mask)))
 
 
 def _hub(g, core, T, topo, other, guests):
     s = T.sem
     _check(topo, core, other)
-    g.sync.dma_start(T.kv[:, 0:KP], T.k[:]).then_inc(s.ldkv, 16)
-    g.scalar.dma_start(T.kv[:, KP:2 * KP], T.v[:]).then_inc(s.ldkv, 16)
-    g.sync.dma_start(T.Q[:, GW:W], T.q[:]).then_inc(s.ldq, 16)
+    g.sync.dma_start(T.kd[:], T.k[:]).then_inc(s.ldkd, 16)
+    g.scalar.dma_start(T.vo[:], T.v[:]).then_inc(s.ldv, 16)
+    g.sync.dma_start(T.ko[:], T.k[:]).then_inc(s.ldk, 16)
+    g.scalar.dma_start(T.Qo[:], T.q[:]).then_inc(s.ldq, 16)
     g.vector.memset(T.zero[:], 0.0).then_inc(s.zs, 1)
 
     rid, pid, _ = topo.addr(other)
     mask = topo.mask(core, other)
-    n_kv = len(_engines(mask))
-    g.wait_ge(s.ldkv, 32)
-    g.remote_dma(T.kvo[:], T.kv[:], s.kvarr, s.sent, pid, rid, mask)
+    n_out = len(_engines(mask))
+    n_in = len(_engines(topo.mask(other, core)))
+    g.wait_ge(s.ldkd, 16)
+    g.remote_dma(T.kx[:], T.kd[:], s.karr, s.sent, pid, rid, mask)
+    g.wait_ge(s.ldv, 16)
+    g.remote_dma(T.vx[:], T.vo[:], s.varr, s.sent, pid, rid, mask)
 
     n_q = sum(len(_engines(topo.mask(c, core))) for c in guests)
     te = g.tensor
-    te.wait_ge(s.ldkv, 32)
-    te.wait_ge(s.ldq, 16)
+    te.wait_ge(s.ldk, 16)
     te.wait_ge(s.qarr, n_q)
-    te.matmul(T.P1[:, 0:W], T.kv[:, 0:KP], T.Q[:], True, True).then_inc(s.m1, 1)
-    te.wait_ge(s.kvarr, len(_engines(topo.mask(other, core))))
-    te.matmul(T.P2[:, 0:W], T.kvo[:, 0:KP], T.Q[:], True, True).then_inc(s.m2, 1)
+    te.matmul(T.P1[:, 0:GW], T.ko[:], T.Q[:], True, True).then_inc(s.m1, 1)
+    te.wait_ge(s.karr, n_in)
+    te.matmul(T.P2a[:, 0:H], T.kx[:], T.Q[:, 0:H], True, True).then_inc(s.m2a, 1)
+    te.matmul(T.P2b[:, 0:H], T.kx[:], T.Q[:, H:GW], True, True).then_inc(s.m2b, 1)
+    te.wait_ge(s.ldv, 16)
     te.wait_ge(s.r1, 1)
-    te.matmul(T.P3[:, 0:W], T.kv[:, KP:2 * KP], T.S1[:], True, False)
-    te.wait_ge(s.r2, 1)
-    te.matmul(T.P3[:, 0:W], T.kvo[:, KP:2 * KP], T.S2[:], False, True).then_inc(s.m3, 1)
+    te.matmul(T.P3a[:, 0:H], T.vo[:], T.S1[:, 0:H], True, False)
+    te.matmul(T.P3b[:, 0:H], T.vo[:], T.S1[:, H:GW], True, False)
+    te.wait_ge(s.varr, n_in)
+    te.wait_ge(s.r2a, 1)
+    te.matmul(T.P3a[:, 0:H], T.vx[:], T.S2a[:], False, True).then_inc(s.m3a, 1)
+    te.wait_ge(s.r2b, 1)
+    te.matmul(T.P3b[:, 0:H], T.vx[:], T.S2b[:], False, True).then_inc(s.m3b, 1)
+    te.wait_ge(s.ldq, 16)
+    te.matmul(T.P5[:, 0:QP], T.ko[:], T.Qo[:], True, True).then_inc(s.m5, 1)
+    te.matmul(T.P5[:, QP:2 * QP], T.kx[:], T.Qo[:], True, True).then_inc(s.m5, 1)
+    te.wait_ge(s.r5, 1)
+    te.matmul(T.P6[:, 0:QP], T.vo[:], T.So[:, 0:QP], True, False)
+    te.matmul(T.P6[:, 0:QP], T.vx[:], T.So[:, QP:2 * QP], False, True).then_inc(s.m6, 1)
 
     ve = g.vector
     ve.wait_ge(s.zs, 1)
     ve.wait_ge(s.m1, 1)
-    ve.tensor_tensor(T.S1[:], T.P1[:, 0:W], T.zero[:], AluOpType.max).then_inc(s.r1, 1)
-    ve.wait_ge(s.m2, 1)
-    ve.tensor_tensor(T.S2[:], T.P2[:, 0:W], T.zero[:], AluOpType.max).then_inc(s.r2, 1)
-    ve.wait_ge(s.m3, 1)
-    ve.tensor_copy(T.Ob[:], T.P3[:, 0:GW]).then_inc(s.c1, 1)
-    ve.tensor_copy(T.Oown[:], T.P3[:, GW:W]).then_inc(s.c2, 1)
+    ve.tensor_tensor(T.S1[:], T.P1[:, 0:GW], T.zero[:], AluOpType.max).then_inc(s.r1, 1)
+    ve.wait_ge(s.m2a, 1)
+    ve.tensor_tensor(T.S2a[:], T.P2a[:, 0:H], T.zero[:, 0:H], AluOpType.max).then_inc(s.r2a, 1)
+    ve.wait_ge(s.m2b, 1)
+    ve.tensor_tensor(T.S2b[:], T.P2b[:, 0:H], T.zero[:, 0:H], AluOpType.max).then_inc(s.r2b, 1)
+    ve.wait_ge(s.m3a, 1)
+    ve.tensor_copy(T.Oa[:], T.P3a[:, 0:H]).then_inc(s.c1a, 1)
+    ve.wait_ge(s.m3b, 1)
+    ve.tensor_copy(T.Obb[:], T.P3b[:, 0:H]).then_inc(s.c1b, 1)
+    ve.wait_ge(s.m5, 2)
+    ve.tensor_tensor(T.So[:], T.P5[:, 0:2 * QP], T.zero[:, 0:2 * QP], AluOpType.max).then_inc(s.r5, 1)
+    ve.wait_ge(s.m6, 1)
+    ve.tensor_copy(T.Oown[:], T.P6[:, 0:QP]).then_inc(s.c2, 1)
 
     common = topo.mask(core, guests[0])
     for c in guests:
         _check(topo, core, c)
         common &= topo.mask(core, c)
     engines = _engines(common)
-    per = _return_engines(topo, core, guests)
-    transfers = []
-    for i, c in enumerate(guests):
-        rid, pid, _ = topo.addr(c)
-        transfers.append(RemoteDMATransfer(dst_ids=[DstId(rid=rid, pnc=pid)],
-                                           dma_engine_mask=_bits(engines[i * per:(i + 1) * per]),
-                                           remote_sem=s.oarr,
-                                           src=T.Ob[:, i * QP:(i + 1) * QP], dst=T.oland[:]))
-    g.wait_ge(s.c1, 1)
-    g.remote_dma_fused(transfers, local_sem=s.sent)
+    per = _return_engines(topo, core, guests[0])
+    for part, (buf, sem) in enumerate(((T.Oa, s.c1a), (T.Obb, s.c1b))):
+        transfers = []
+        for i, c in enumerate(guests[part * PART:(part + 1) * PART]):
+            rid, pid, _ = topo.addr(c)
+            transfers.append(RemoteDMATransfer(dst_ids=[DstId(rid=rid, pnc=pid)],
+                                               dma_engine_mask=_bits(engines[i * per:(i + 1) * per]),
+                                               remote_sem=s.oarr,
+                                               src=buf[:, i * QP:(i + 1) * QP], dst=T.oland[:]))
+        g.wait_ge(sem, 1)
+        g.remote_dma_fused(transfers, local_sem=s.sent)
 
     g.sync.wait_ge(s.c2, 1)
     g.sync.dma_start(T.y[:], T.Oown[:]).then_inc(s.st, 16)
     g.sync.wait_ge(s.st, 16)
-    g.wait_ge(s.sent, n_kv + per * len(guests))
+    g.wait_ge(s.sent, 2 * n_out + per * len(guests))
 
 
 def rank_program(g, core, T, topo):

from concourse.bass import DstId, RemoteDMATransfer
from concourse.mybir import AluOpType

QP = 32
KP = 128
GUESTS = 4
PART = GUESTS // 2
GW = GUESTS * QP
H = GW // 2

SCRATCH = {
    "qd": ("dram", [128, QP], "bfloat16"),
    "oland": ("dram", [128, QP], "bfloat16"),
    "kd": ("dram", [128, KP], "bfloat16"),
    "ko": ("sbuf", [128, KP], "bfloat16"),
    "vo": ("sbuf", [128, KP], "bfloat16"),
    "kx": ("sbuf", [128, KP], "bfloat16"),
    "vx": ("sbuf", [128, KP], "bfloat16"),
    "Q": ("sbuf", [128, GW], "bfloat16"),
    "Qo": ("sbuf", [128, QP], "bfloat16"),
    "zero": ("sbuf", [128, GW], "float32"),
    "S1": ("sbuf", [128, GW], "bfloat16"),
    "S2a": ("sbuf", [128, H], "bfloat16"),
    "S2b": ("sbuf", [128, H], "bfloat16"),
    "So": ("sbuf", [128, 2 * QP], "bfloat16"),
    "Oa": ("sbuf", [128, H], "bfloat16"),
    "Obb": ("sbuf", [128, H], "bfloat16"),
    "Oown": ("sbuf", [128, QP], "bfloat16"),
    "P1": ("psum", [128, 512], "float32"),
    "P2a": ("psum", [128, 512], "float32"),
    "P2b": ("psum", [128, 512], "float32"),
    "P3a": ("psum", [128, 512], "float32"),
    "P3b": ("psum", [128, 512], "float32"),
    "P5": ("psum", [128, 512], "float32"),
    "P6": ("psum", [128, 512], "float32"),
}
SEMAPHORES = ["ldkd", "ldk", "ldv", "ldq", "qarr", "karr", "varr", "oarr", "sent", "st", "zs",
              "m1", "m2a", "m2b", "m3a", "m3b", "m5", "m6", "r1", "r2a", "r2b", "r5", "c1a", "c1b", "c2"]


def _engines(mask):
    return [b for b in range(mask.bit_length()) if (mask >> b) & 1]


def _bits(engines):
    m = 0
    for b in engines:
        m |= 1 << b
    return m


def _pow2_floor(n):
    p = 1
    while 2 * p <= n:
        p *= 2
    return p


def _hops(topo, a, b):
    ca, cb = topo.chip(a), topo.chip(b)
    if ca == cb:
        return 0
    if topo.mates(ca, cb) or topo.same_plane(ca, cb):
        return 1
    return 2


def _plan(T, topo):
    hubs = [T.cores[j] for j in T.tables["MEM"]]
    guests = {h: [] for h in hubs}
    rest = [c for c in T.cores if c not in hubs]
    near = [c for c in rest if len({_hops(topo, c, h) for h in hubs}) > 1]
    for c in near:
        guests[min(hubs, key=lambda h: _hops(topo, c, h))].append(c)
    even = sorted([c for c in rest if c not in near], key=lambda c: _hops(topo, c, hubs[0]))
    for c in even:
        guests[min(hubs, key=lambda h: len(guests[h]))].append(c)
    for h in hubs:
        guests[h].sort(key=lambda c: -_hops(topo, c, h))
    return hubs, guests


def _check(topo, src, dst):
    if not topo.may_write(src, dst):
        raise ValueError("core %d may not write to core %d" % (src, dst))


def _return_engines(topo, hub, dst):
    return _pow2_floor(len(_engines(topo.mask(hub, dst))) // PART)


def _guest(g, core, T, topo, hub, slot):
    _check(topo, core, hub)
    rid, pid, _ = topo.addr(hub)
    mask = topo.mask(core, hub)
    g.sync.dma_start(T.qd[:], T.q[:]).then_inc(T.sem.ldq, 16)
    g.wait_ge(T.sem.ldq, 16)
    g.remote_dma(T.Q[:, slot * QP:(slot + 1) * QP], T.qd[:], T.sem.qarr, T.sem.sent, pid, rid, mask)
    g.sync.wait_ge(T.sem.oarr, _return_engines(topo, hub, core))
    g.sync.dma_start(T.y[:], T.oland[:]).then_inc(T.sem.st, 16)
    g.sync.wait_ge(T.sem.st, 16)
    g.wait_ge(T.sem.sent, len(_engines(mask)))


def _hub(g, core, T, topo, other, guests):
    s = T.sem
    _check(topo, core, other)
    g.sync.dma_start(T.kd[:], T.k[:]).then_inc(s.ldkd, 16)
    g.scalar.dma_start(T.vo[:], T.v[:]).then_inc(s.ldv, 16)
    g.sync.dma_start(T.ko[:], T.k[:]).then_inc(s.ldk, 16)
    g.scalar.dma_start(T.Qo[:], T.q[:]).then_inc(s.ldq, 16)
    g.vector.memset(T.zero[:], 0.0).then_inc(s.zs, 1)

    rid, pid, _ = topo.addr(other)
    mask = topo.mask(core, other)
    n_out = len(_engines(mask))
    n_in = len(_engines(topo.mask(other, core)))
    g.wait_ge(s.ldkd, 16)
    g.remote_dma(T.kx[:], T.kd[:], s.karr, s.sent, pid, rid, mask)
    g.wait_ge(s.ldv, 16)
    g.remote_dma(T.vx[:], T.vo[:], s.varr, s.sent, pid, rid, mask)

    n_q = sum(len(_engines(topo.mask(c, core))) for c in guests)
    te = g.tensor
    te.wait_ge(s.ldk, 16)
    te.wait_ge(s.qarr, n_q)
    te.matmul(T.P1[:, 0:GW], T.ko[:], T.Q[:], True, True).then_inc(s.m1, 1)
    te.wait_ge(s.karr, n_in)
    te.matmul(T.P2a[:, 0:H], T.kx[:], T.Q[:, 0:H], True, True).then_inc(s.m2a, 1)
    te.matmul(T.P2b[:, 0:H], T.kx[:], T.Q[:, H:GW], True, True).then_inc(s.m2b, 1)
    te.wait_ge(s.ldv, 16)
    te.wait_ge(s.r1, 1)
    te.matmul(T.P3a[:, 0:H], T.vo[:], T.S1[:, 0:H], True, False)
    te.matmul(T.P3b[:, 0:H], T.vo[:], T.S1[:, H:GW], True, False)
    te.wait_ge(s.varr, n_in)
    te.wait_ge(s.r2a, 1)
    te.matmul(T.P3a[:, 0:H], T.vx[:], T.S2a[:], False, True).then_inc(s.m3a, 1)
    te.wait_ge(s.r2b, 1)
    te.matmul(T.P3b[:, 0:H], T.vx[:], T.S2b[:], False, True).then_inc(s.m3b, 1)
    te.wait_ge(s.ldq, 16)
    te.matmul(T.P5[:, 0:QP], T.ko[:], T.Qo[:], True, True).then_inc(s.m5, 1)
    te.matmul(T.P5[:, QP:2 * QP], T.kx[:], T.Qo[:], True, True).then_inc(s.m5, 1)
    te.wait_ge(s.r5, 1)
    te.matmul(T.P6[:, 0:QP], T.vo[:], T.So[:, 0:QP], True, False)
    te.matmul(T.P6[:, 0:QP], T.vx[:], T.So[:, QP:2 * QP], False, True).then_inc(s.m6, 1)

    ve = g.vector
    ve.wait_ge(s.zs, 1)
    ve.wait_ge(s.m1, 1)
    ve.tensor_tensor(T.S1[:], T.P1[:, 0:GW], T.zero[:], AluOpType.max).then_inc(s.r1, 1)
    ve.wait_ge(s.m2a, 1)
    ve.tensor_tensor(T.S2a[:], T.P2a[:, 0:H], T.zero[:, 0:H], AluOpType.max).then_inc(s.r2a, 1)
    ve.wait_ge(s.m2b, 1)
    ve.tensor_tensor(T.S2b[:], T.P2b[:, 0:H], T.zero[:, 0:H], AluOpType.max).then_inc(s.r2b, 1)
    ve.wait_ge(s.m3a, 1)
    ve.tensor_copy(T.Oa[:], T.P3a[:, 0:H]).then_inc(s.c1a, 1)
    ve.wait_ge(s.m3b, 1)
    ve.tensor_copy(T.Obb[:], T.P3b[:, 0:H]).then_inc(s.c1b, 1)
    ve.wait_ge(s.m5, 2)
    ve.tensor_tensor(T.So[:], T.P5[:, 0:2 * QP], T.zero[:, 0:2 * QP], AluOpType.max).then_inc(s.r5, 1)
    ve.wait_ge(s.m6, 1)
    ve.tensor_copy(T.Oown[:], T.P6[:, 0:QP]).then_inc(s.c2, 1)

    common = topo.mask(core, guests[0])
    for c in guests:
        _check(topo, core, c)
        common &= topo.mask(core, c)
    engines = _engines(common)
    per = _return_engines(topo, core, guests[0])
    for part, (buf, sem) in enumerate(((T.Oa, s.c1a), (T.Obb, s.c1b))):
        transfers = []
        for i, c in enumerate(guests[part * PART:(part + 1) * PART]):
            rid, pid, _ = topo.addr(c)
            transfers.append(RemoteDMATransfer(dst_ids=[DstId(rid=rid, pnc=pid)],
                                               dma_engine_mask=_bits(engines[i * per:(i + 1) * per]),
                                               remote_sem=s.oarr,
                                               src=buf[:, i * QP:(i + 1) * QP], dst=T.oland[:]))
        g.wait_ge(sem, 1)
        g.remote_dma_fused(transfers, local_sem=s.sent)

    g.sync.wait_ge(s.c2, 1)
    g.sync.dma_start(T.y[:], T.Oown[:]).then_inc(s.st, 16)
    g.sync.wait_ge(s.st, 16)
    g.wait_ge(s.sent, 2 * n_out + per * len(guests))


def rank_program(g, core, T, topo):
    if T.rank_of(core) is None:
        return
    hubs, guests = _plan(T, topo)
    if core in hubs:
        _hub(g, core, T, topo, hubs[1 - hubs.index(core)], guests[core])
    else:
        for h in hubs:
            if core in guests[h]:
                _guest(g, core, T, topo, h, guests[h].index(core))
